import numpy as np
import ml_dtypes


def mxq(x, axis, fmt="e4m3"):
    dtype, down = {"e4m3": (ml_dtypes.float8_e4m3fn, 7), "e5m2": (ml_dtypes.float8_e5m2, 14)}[fmt]
    v = np.moveaxis(np.asarray(x, np.float32).astype(ml_dtypes.bfloat16).astype(np.float64), axis, -1)
    blocks = v.reshape(v.shape[:-1] + (-1, 32))
    amax = np.abs(blocks).max(-1, keepdims=True)
    byte = np.maximum(np.where(amax > 0, np.frexp(amax)[1] - 1 + 127, 0) - down, 1)
    scale = np.exp2(byte - 127.0)
    codes = (blocks / scale).astype(np.float32).astype(dtype).astype(np.float64)
    return np.moveaxis((codes * scale).reshape(v.shape), -1, axis)


WIDE = False


def mx_kscale(k):
    if not WIDE:
        return np.ones(k)
    levels = np.array([30, -30])
    if k % 512:
        return np.exp2(np.random.permutation(np.resize(levels, k // 32))).repeat(32)
    a = np.empty((k // 512, 16))
    for p in range(k // 512):
        a[p, :8] = np.random.permutation(np.resize(levels, 8))
        for g in range(8):
            far = levels[np.abs(levels - a[p, g]) >= 10]
            a[p, g + 8] = far[np.random.randint(len(far))]
    return np.exp2(a.ravel()).repeat(32)


def f64(x):
    return np.asarray(x).astype(np.float64)


E2M1 = np.array([0.0, 0.5, 1.0, 1.5, 2.0, 3.0, 4.0, 6.0, -0.0, -0.5, -1.0, -1.5, -2.0, -3.0, -4.0, -6.0])


def pack_weight(w, fmt):
    k, n = w.shape
    w = f64(np.asarray(w, np.float32).astype(ml_dtypes.bfloat16)).reshape(k // 32, 32, n)
    amax = np.abs(w).max(1)
    if fmt == "e4m3":
        byte = np.frexp(amax)[1] - 1 + 127 - 7
    else:
        mant, ex = np.frexp(amax / 6.0)
        byte = np.where(mant > 0.5, ex, ex - 1) + 127
    byte = np.clip(np.where(amax > 0, byte, 1), 1, 254)
    scaled = (w * np.exp2(127.0 - byte)[:, None, :]).reshape(k, n).astype(np.float32)
    by_word = np.ascontiguousarray(scaled.reshape(k // 512, 128, 4, n).transpose(0, 1, 3, 2))
    if fmt == "e4m3":
        words = by_word.astype(ml_dtypes.float8_e4m3fn).view(np.uint8)
    else:
        c = by_word.astype(ml_dtypes.float4_e2m1fn).view(np.uint8) & 0xF
        words = (c[..., 0::2] | (c[..., 1::2] << 4)).reshape(k // 512, 128, 2 * n)
    return np.ascontiguousarray(words), np.ascontiguousarray(byte.astype(np.uint8).reshape(k // 512, 16, n))


def unpack_weight(words, scales, fmt):
    g, _, n = scales.shape
    words = np.ascontiguousarray(words).reshape(g, 128, n, -1)
    if fmt == "e4m3":
        vals = words.view(ml_dtypes.float8_e4m3fn).astype(np.float64)
    else:
        nib = np.empty((g, 128, n, 4), np.uint8)
        nib[..., 0::2] = words & 0xF
        nib[..., 1::2] = words >> 4
        vals = E2M1[nib]
    vals = vals * np.repeat(np.exp2(scales.astype(np.float64) - 127.0), 8, axis=1)[..., None]
    return vals.transpose(0, 1, 3, 2).reshape(g * 512, n)


def bf(x):
    return np.asarray(x, np.float32).astype(ml_dtypes.bfloat16)


def planes(Y):
    r, m = Y.shape
    b = f64(bf(Y)).reshape(r // 32, 32, m)
    amax = np.abs(b).max(1)
    byte = np.clip(np.where(amax > 0, np.frexp(amax)[1] - 1 + 127 - 7, 1), 1, 254)
    codes = (b * np.exp2(127.0 - byte)[:, None, :]).reshape(r, m).astype(np.float32).astype(ml_dtypes.float8_e4m3fn).view(np.uint8)
    words = codes.reshape(r // 512, 128, 4, m).transpose(0, 1, 3, 2)
    return np.ascontiguousarray(words), np.ascontiguousarray(byte.astype(np.uint8).reshape(r // 512, 16, m))


K, N, T, S = 512, 512, 1024, 1024


def setup_inputs():
    n = np.random.standard_normal
    ft = mx_kscale(T)
    fs = mx_kscale(S)
    sap = pack_weight(n((S, K)) / fs[:, None], "e2m1")
    sbp = pack_weight(n((S, N)) * fs[:, None], "e4m3")
    return {
        "xa": (n((K, T))).astype(np.float32),
        "xb": (n((N, T))).astype(np.float32),
        "ra": (np.random.uniform(0.5, 1.5, (1, T)) * ft).astype(np.float32),
        "rb": (np.random.uniform(0.5, 1.5, (1, T)) / ft).astype(np.float32),
        "sa_words": sap[0],
        "sa_scales": sap[1],
        "sb_words": sbp[0],
        "sb_scales": sbp[1],
    }


def reference(xa, xb, ra, rb, sa_words, sa_scales, sb_words, sb_scales):
    sau = unpack_weight(sa_words, sa_scales, "e2m1")
    sbu = unpack_weight(sb_words, sb_scales, "e4m3")
    da = (f64(xa) - np.mean(f64(xa), axis=1, keepdims=True)) * f64(ra)
    db = (f64(xb) - np.mean(f64(xb), axis=1, keepdims=True)) * f64(rb)
    ta = da.T
    tb = db.T
    taq = mxq(ta, 0, "e4m3")
    tbq = mxq(tb, 0, "e5m2")
    v = taq.T @ tbq + sau.T @ sbu
    y = 0.03 * v
    words, scales = planes(y)
    return y, words, scales

@@ -1,0 +1,325 @@
+from contextlib import ExitStack
+
+import concourse.mybir as mybir
+from concourse.masks import make_identity
+
+K, N, T, S = 512, 512, 1024, 1024
+FLOPS = 2 * K * N * (T + S)
+
+F32 = mybir.dt.float32
+BF16 = mybir.dt.bfloat16
+I32 = mybir.dt.int32
+U32 = mybir.dt.uint32
+U8 = mybir.dt.uint8
+E4M3 = mybir.dt.float8_e4m3fn_x4
+E5M2 = mybir.dt.float8_e5m2_x4
+E2M1 = mybir.dt.float4_e2m1fn_x4
+ALU = mybir.AluOpType
+ACT = mybir.ActivationFunctionType
+
+P = 128
+PASS = 512
+OUT_SCALE = 0.03
+VECTOR_MEAN_COLS = {0: 512, 4: 1024, 7: 512}
+
+
+def tile_mix_covariances_of_two_stores_pl_kernel(
+    tc, xa, xb, ra, rb, sa_words, sa_scales, sb_words, sb_scales, out_0, out_1, out_2
+):
+    nc = tc.nc
+    with ExitStack() as ctx:
+        sb = ctx.enter_context(tc.tile_pool(name="sb", bufs=1))
+        ps = ctx.enter_context(tc.psum_pool(name="ps", bufs=1))
+        ctx.enter_context(tc.manual_schedule())
+
+        def sbt(name, cols, dt):
+            return sb.tile([P, cols], dt, name=name, align_bytes=64)
+
+        bank = [ps.tile([P, 512], F32, name="bank%d" % j) for j in range(8)]
+        ident = sbt("ident", P, F32)
+        warm = sbt("warm", 16, F32)
+        rcol = [sbt("rcol%d" % j, 16, F32) for j in range(2)]
+        x = [sbt("x%d" % i, T, F32) for i in range(8)]
+        d = [[sbt("d%d_%d" % (i, g), PASS, BF16) for g in range(2)] for i in range(8)]
+        junk_s = [sbt("junk_s%d" % j, T, BF16) for j in range(2)]
+        junk_v = sbt("junk_v", PASS, BF16)
+        part_s = [sbt("part_s%d" % i, 1, F32) for i in range(8)]
+        part_v = [sbt("part_v%d" % i, 1, F32) for i in range(8)]
+        mean = [sbt("mean%d" % i, 1, F32) for i in range(8)]
+        gb = [sbt("gb%d" % j, 2048, BF16) for j in range(2)]
+        ga = [[sbt("ga%d_%d" % (r, g), 512, BF16) for g in range(2)] if r == 3 else sbt("ga%d" % r, 1024, BF16) for r in range(4)]
+        b_codes = sbt("b_codes", 1024, U32)
+        b_scale = sbt("b_scale", 1024, U8)
+        a_codes = [sbt("a_codes%d" % r, 256, U32) for r in range(4)]
+        a_scale = [sbt("a_scale%d" % r, 256, U8) for r in range(4)]
+        sa_raw = sbt("sa_raw", 2048, U8)
+        sa_dealt = sbt("sa_dealt", 2048, U8)
+        sas_raw = sbt("sas_raw", 1024, U8)
+        sas_dealt = sbt("sas_dealt", 1024, U8)
+        sbw = sbt("sbw", 1024, U32)
+        sbs = sbt("sbs", 1024, U8)
+        y = sbt("y", 2048, F32)
+        yb = sbt("yb", 2048, BF16)
+        o_codes = sbt("o_codes", 512, U32)
+        o_scale = sbt("o_scale", 512, U8)
+
+        r_bank = [[bank[0], bank[1]], [bank[2], bank[3]]]
+        stage = [bank[4], bank[5], bank[6], bank[7], bank[6], bank[7], bank[6]]
+        last_stage = [bank[7], bank[2]]
+        acc = [bank[4], bank[5], bank[0], bank[1]]
+
+        xa_dealt = xa.rearrange("(p r) t -> r p t", r=4)
+        out_dealt = out_0.rearrange("(p r) n -> r p n", r=4)
+
+        def rows(i):
+            return xb[P * i : P * (i + 1), :] if i < 4 else xa_dealt[i - 4]
+
+        def load_x(i, lo=0, hi=T):
+            nc.sync.dma_start(out=x[i][:, lo:hi], in_=rows(i)[:, lo:hi])
+
+        def load_r(j, r):
+            nc.sync.dma_start(
+                out=rcol[j][:].rearrange("p (g c) -> p g c", g=2)[:, :, 0:4],
+                in_=r.rearrange("o (g p c) -> p (o g) c", g=2, c=4),
+            )
+
+        def load_scales(eng, plane, scales):
+            for q in range(4):
+                eng.dma_start(
+                    out=plane[32 * q : 32 * q + 4, :].bitcast(I32).rearrange("q (z c) -> q z c", z=2),
+                    in_=scales[:, 4 * q : 4 * q + 4, :].bitcast(I32).rearrange("z q c -> q z c"),
+                )
+
+        def spread_r(j):
+            for g in range(2):
+                for c in range(4):
+                    col = rcol[j][:, 8 * g + c : 8 * g + c + 1]
+                    nc.tensor.transpose(r_bank[j][g][:, P * c : P * (c + 1)], col.to_broadcast([P, P]), ident[:])
+
+        def mean_scalar(i):
+            cols = T - VECTOR_MEAN_COLS.get(i, 0)
+            if cols:
+                dst = mean[i] if cols == T else part_s[i]
+                nc.scalar.activation(
+                    out=junk_s[i % 2][:, 0:cols], in_=x[i][:, 0:cols], func=ACT.Copy, scale=1.0 / T, accum_out=dst[:]
+                )
+
+        def mean_vector(i):
+            v = VECTOR_MEAN_COLS[i]
+            lo = T - v
+            nc.vector.scalar_tensor_tensor(
+                out=junk_v[:, 0 : v // 2], in0=x[i][:, lo : lo + v // 2], scalar=1.0, in1=x[i][:, lo + v // 2 : T],
+                op0=ALU.mult, op1=ALU.add, accum_out=part_v[i][:],
+            )
+
+        def mean_join(i):
+            if VECTOR_MEAN_COLS[i] == T:
+                nc.vector.tensor_scalar(out=mean[i][:], in0=part_v[i][:], scalar1=1.0 / T, scalar2=None, op0=ALU.mult)
+            else:
+                nc.vector.tensor_scalar(
+                    out=mean[i][:], in0=part_v[i][:], scalar1=1.0 / T, scalar2=part_s[i][:], op0=ALU.mult, op1=ALU.add
+                )
+
+        def centre(i, g):
+            nc.vector.scalar_tensor_tensor(
+                out=d[i][g][:].rearrange("p (n c) -> p n c", c=4),
+                in0=x[i][:, PASS * g : PASS * (g + 1)].rearrange("p (n c) -> p n c", c=4),
+                scalar=mean[i][:],
+                in1=r_bank[i // 4][g][:].rearrange("p (c n) -> p n c", c=4),
+                op0=ALU.subtract,
+                op1=ALU.mult,
+            )
+
+        def turn(i, g):
+            words = d[i][g][:].bitcast(F32)
+            for u in range(2):
+                if i < 7:
+                    dst = stage[i][:, P * (2 * g + u) : P * (2 * g + u + 1)]
+                else:
+                    dst = last_stage[g][:, P * u : P * (u + 1)]
+                nc.tensor.transpose(dst, words[:, u:256:2], ident[:])
+
+        def copy_out(i):
+            src = stage[i][:].rearrange("p (g u k) -> p g k u", g=2, u=2)
+            if i < 4:
+                dst = gb[i // 2][:].bitcast(F32).rearrange("p (g k u) -> p g k u", g=2, u=2)
+                dst = dst[:, :, P * (i % 2) : P * (i % 2 + 1), :]
+            else:
+                dst = ga[i - 4][:].bitcast(F32).rearrange("p (g k u) -> p g k u", g=2, u=2)
+            nc.scalar.copy(out=dst, in_=src)
+
+        def copy_last(g):
+            nc.scalar.copy(
+                out=ga[3][g][:].bitcast(F32).rearrange("p (k u) -> p k u", u=2),
+                in_=last_stage[g][:, 0:256].rearrange("p (u k) -> p k u", u=2),
+            )
+
+        def quant_b(pair):
+            for g in range(2):
+                cols = slice(512 * g + 256 * pair, 512 * g + 256 * (pair + 1))
+                nc.vector.quantize_mx(
+                    out=b_codes[:, cols].bitcast(E5M2), scales=b_scale[:, cols], in_=gb[pair][:, 1024 * g : 1024 * (g + 1)]
+                )
+
+        def quant_a(r):
+            nc.vector.quantize_mx(out=a_codes[r][:].bitcast(E4M3), scales=a_scale[r][:], in_=ga[r][:])
+
+        def quant_last(g):
+            cols = slice(P * g, P * (g + 1))
+            nc.vector.quantize_mx(out=a_codes[3][:, cols].bitcast(E4M3), scales=a_scale[3][:, cols], in_=ga[3][g][:])
+
+        def stored(r):
+            for z in range(2):
+                j = 4 * z + r
+                nc.tensor.matmul_mx(
+                    out=acc[r][:],
+                    lhsT=sa_dealt[:, 256 * j : 256 * (j + 1)].bitcast(E2M1),
+                    lhsT_scale=sas_dealt[:, P * j : P * (j + 1)],
+                    rhs=sbw[:, 512 * z : 512 * (z + 1)].bitcast(E4M3),
+                    rhs_scale=sbs[:, 512 * z : 512 * (z + 1)],
+                    start=(z == 0),
+                    stop=False,
+                )
+
+        def fresh(r, g):
+            nc.tensor.matmul_mx(
+                out=acc[r][:],
+                lhsT=a_codes[r][:, P * g : P * (g + 1)].bitcast(E4M3),
+                lhsT_scale=a_scale[r][:, P * g : P * (g + 1)],
+                rhs=b_codes[:, 512 * g : 512 * (g + 1)].bitcast(E5M2),
+                rhs_scale=b_scale[:, 512 * g : 512 * (g + 1)],
+                start=False,
+                stop=(g == 1),
+            )
+
+        def evac_scalar(r, lo=0, hi=N):
+            nc.scalar.activation(out=y[:, N * r + lo : N * r + hi], in_=acc[r][:, lo:hi], func=ACT.Copy, scale=OUT_SCALE)
+
+        def evac_vector(r):
+            nc.vector.tensor_scalar(out=y[:, N * r : N * (r + 1)], in0=acc[r][:], scalar1=OUT_SCALE, scalar2=None, op0=ALU.mult)
+
+        def store_y(r):
+            nc.sync.dma_start(out=out_dealt[r], in_=y[:, N * r : N * (r + 1)])
+
+        def weave(copy, lo, hi):
+            copy(
+                out=yb[:, 4 * lo : 4 * hi].rearrange("p (c i r) -> p c r i", i=4, r=4),
+                in_=y[:].rearrange("p (r n) -> p r n", r=4)[:, :, lo:hi].rearrange("p r (c i) -> p c r i", i=4),
+            )
+
+        def quant_out(lo, hi):
+            nc.vector.quantize_mx(out=o_codes[:, lo:hi].bitcast(E4M3), scales=o_scale[:, lo:hi], in_=yb[:, 4 * lo : 4 * hi])
+
+        def store_codes(lo, hi):
+            nc.sync.dma_start(
+                out=out_1[0].rearrange("p n r -> p (n r)")[:, 4 * lo : 4 * hi].bitcast(I32), in_=o_codes[:, lo:hi].bitcast(I32)
+            )
+
+        nc.vector.memset(warm[:, 0:1], 0.0)
+        nc.vector.memset(sas_raw[:].bitcast(U32), 0)
+        nc.vector.memset(sbs[:].bitcast(U32), 0)
+        nc.scalar.activation(out=warm[:, 8:9], in_=warm[:, 0:1], func=ACT.Copy, scale=1.0)
+        make_identity(nc, ident[:])
+        load_r(0, rb)
+        nc.sync.dma_start(
+            out=sa_raw[:].bitcast(I32).rearrange("p (z c) -> p z c", z=2), in_=sa_words.bitcast(I32).rearrange("z p c -> p z c")
+        )
+        load_x(0, 0, 512)
+        load_x(0, 512, T)
+        load_r(1, ra)
+        for i in range(1, 4):
+            load_x(i)
+        load_scales(nc.sync, sas_raw, sa_scales)
+        load_x(4)
+        load_scales(nc.sync, sbs, sb_scales)
+        nc.sync.dma_start(
+            out=sbw[:].bitcast(I32).rearrange("p (z c) -> p z c", z=2),
+            in_=sb_words.rearrange("z p n t -> p z (n t)").bitcast(I32),
+        )
+        load_x(5)
+        load_x(6)
+        load_x(7, 0, 512)
+        load_x(7, 512, T)
+
+        spread_r(0)
+        nc.vector.tensor_copy(
+            out=sa_dealt[:].rearrange("p (z r m b) -> p z r m b", z=2, r=4, b=2),
+            in_=sa_raw[:].rearrange("p (z m r b) -> p z r m b", z=2, r=4, b=2),
+        )
+        mean_scalar(0)
+        mean_vector(0)
+        mean_join(0)
+        spread_r(1)
+
+        def tile_front(i):
+            for g in range(2):
+                centre(i, g)
+                turn(i, g)
+
+        mean_scalar(1)
+        tile_front(0)
+        mean_scalar(2)
+        tile_front(1)
+        copy_out(0)
+        mean_scalar(3)
+        tile_front(2)
+        copy_out(1)
+        tile_front(3)
+        copy_out(2)
+        mean_vector(4)
+        quant_b(0)
+        mean_join(4)
+        nc.vector.tensor_copy(
+            out=sas_dealt[:].rearrange("p (z r m) -> p z r m", z=2, r=4),
+            in_=sas_raw[:].rearrange("p (z m r) -> p z r m", z=2, r=4),
+        )
+        mean_scalar(5)
+        copy_out(3)
+        tile_front(4)
+        stored(0)
+        stored(1)
+        mean_scalar(6)
+        copy_out(4)
+        tile_front(5)
+        quant_b(1)
+        quant_a(0)
+        fresh(0, 0)
+        fresh(0, 1)
+        stored(2)
+        mean_scalar(7)
+        copy_out(5)
+        tile_front(6)
+        mean_vector(7)
+        quant_a(1)
+        mean_join(7)
+        fresh(1, 0)
+        fresh(1, 1)
+        stored(3)
+        evac_scalar(0)
+        store_y(0)
+        copy_out(6)
+        tile_front(7)
+        evac_scalar(1)
+        store_y(1)
+        quant_a(2)
+        fresh(2, 0)
+        fresh(2, 1)
+        for g in range(2):
+            copy_last(g)
+            quant_last(g)
+            fresh(3, g)
+        evac_vector(2)
+        store_y(2)
+        evac_scalar(3, 0, 256)
+        evac_scalar(3, 256, N)
+        store_y(3)
+        weave(nc.vector.tensor_copy, 0, 256)
+        weave(nc.vector.tensor_copy, 256, 384)
+        weave(nc.scalar.copy, 384, N)
+        quant_out(0, 256)
+        store_codes(0, 256)
+        quant_out(256, N)
+        store_codes(256, N)
+        for q in range(4):
+            eng = nc.scalar if q % 2 else nc.sync
+            eng.dma_start(out=out_2[0, 4 * q : 4 * q + 4, :].bitcast(I32), in_=o_scale[32 * q : 32 * q + 4, :].bitcast(I32))

@@ -20,7 +20,7 @@ ACT = mybir.ActivationFunctionType
 P = 128
 PASS = 512
 OUT_SCALE = 0.03
-VECTOR_MEAN_COLS = {0: 512, 4: 1024, 7: 512}
+VECTOR_MEAN_COLS = {0: 512}
 
 
 def tile_mix_covariances_of_two_stores_pl_kernel(
@@ -38,7 +38,7 @@ def tile_mix_covariances_of_two_stores_pl_kernel(
         bank = [ps.tile([P, 512], F32, name="bank%d" % j) for j in range(8)]
         ident = sbt("ident", P, F32)
         warm = sbt("warm", 16, F32)
-        rcol = [sbt("rcol%d" % j, 16, F32) for j in range(2)]
+        rcol = [sbt("rcol%d" % j, 8, F32) for j in range(2)]
         x = [sbt("x%d" % i, T, F32) for i in range(8)]
         d = [[sbt("d%d_%d" % (i, g), PASS, BF16) for g in range(2)] for i in range(8)]
         junk_s = [sbt("junk_s%d" % j, T, BF16) for j in range(2)]
@@ -46,14 +46,14 @@ def tile_mix_covariances_of_two_stores_pl_kernel(
         part_s = [sbt("part_s%d" % i, 1, F32) for i in range(8)]
         part_v = [sbt("part_v%d" % i, 1, F32) for i in range(8)]
         mean = [sbt("mean%d" % i, 1, F32) for i in range(8)]
-        gb = [sbt("gb%d" % j, 2048, BF16) for j in range(2)]
+        gb = sbt("gb", 4096, BF16)
         ga = [[sbt("ga%d_%d" % (r, g), 512, BF16) for g in range(2)] if r == 3 else sbt("ga%d" % r, 1024, BF16) for r in range(4)]
         b_codes = sbt("b_codes", 1024, U32)
         b_scale = sbt("b_scale", 1024, U8)
         a_codes = [sbt("a_codes%d" % r, 256, U32) for r in range(4)]
         a_scale = [sbt("a_scale%d" % r, 256, U8) for r in range(4)]
         sa_raw = sbt("sa_raw", 2048, U8)
-        sa_dealt = sbt("sa_dealt", 2048, U8)
+        sa_dealt = [sbt("sa_dealt%d" % r, 512, U8) for r in range(4)]
         sas_raw = sbt("sas_raw", 1024, U8)
         sas_dealt = sbt("sas_dealt", 1024, U8)
         sbw = sbt("sbw", 1024, U32)
@@ -64,8 +64,8 @@ def tile_mix_covariances_of_two_stores_pl_kernel(
         o_scale = sbt("o_scale", 512, U8)
 
         r_bank = [[bank[0], bank[1]], [bank[2], bank[3]]]
-        stage = [bank[4], bank[5], bank[6], bank[7], bank[6], bank[7], bank[6]]
-        last_stage = [bank[7], bank[2]]
+        stage = [bank[4], bank[5], bank[6], bank[7], bank[4], bank[6], bank[7]]
+        last_stage = [bank[6], bank[2]]
         acc = [bank[4], bank[5], bank[0], bank[1]]
 
         xa_dealt = xa.rearrange("(p r) t -> r p t", r=4)
@@ -78,22 +78,56 @@ def tile_mix_covariances_of_two_stores_pl_kernel(
             nc.sync.dma_start(out=x[i][:, lo:hi], in_=rows(i)[:, lo:hi])
 
         def load_r(j, r):
+            nc.sync.dma_start(out=rcol[j][:], in_=r.rearrange("o (p c) -> (o p) c", c=8))
+
+        def load_scales(plane, scales, q):
             nc.sync.dma_start(
-                out=rcol[j][:].rearrange("p (g c) -> p g c", g=2)[:, :, 0:4],
-                in_=r.rearrange("o (g p c) -> p (o g) c", g=2, c=4),
+                out=plane[32 * q : 32 * q + 4, :].bitcast(I32).rearrange("q (z c) -> q z c", z=2),
+                in_=scales[:, 4 * q : 4 * q + 4, :].bitcast(I32).rearrange("z q c -> q z c"),
             )
 
-        def load_scales(eng, plane, scales):
-            for q in range(4):
-                eng.dma_start(
-                    out=plane[32 * q : 32 * q + 4, :].bitcast(I32).rearrange("q (z c) -> q z c", z=2),
-                    in_=scales[:, 4 * q : 4 * q + 4, :].bitcast(I32).rearrange("z q c -> q z c"),
-                )
+        def deal_words(eng, r):
+            eng.tensor_copy(
+                out=sa_dealt[r][:].rearrange("p (m b) -> p m b", b=2),
+                in_=sa_raw[:].rearrange("p (m r b) -> p r m b", r=4, b=2)[:, r],
+            )
+
+        def deal_scales(eng):
+            eng.tensor_copy(
+                out=sas_dealt[:].rearrange("p (z r m) -> p z r m", z=2, r=4),
+                in_=sas_raw[:].rearrange("p (z m r) -> p z r m", z=2, r=4),
+            )
+
+        def load_sa():
+            nc.sync.dma_start(
+                out=sa_raw[:].bitcast(I32).rearrange("p (z c) -> p z c", z=2),
+                in_=sa_words.bitcast(I32).rearrange("z p c -> p z c"),
+            )
+
+        def load_sb():
+            nc.sync.dma_start(
+                out=sbw[:].bitcast(I32).rearrange("p (z c) -> p z c", z=2),
+                in_=sb_words.rearrange("z p n t -> p z (n t)").bitcast(I32),
+            )
+
+        def centre_both(i):
+            for u in range(2):
+                centre(i, u)
+
+        def turn_both(i):
+            for u in range(2):
+                turn(i, u)
+
+        def tile_front(i):
+            for u in range(2):
+                centre(i, u)
+            for u in range(2):
+                turn(i, u)
 
         def spread_r(j):
             for g in range(2):
                 for c in range(4):
-                    col = rcol[j][:, 8 * g + c : 8 * g + c + 1]
+                    col = rcol[j][:, 4 * g + c : 4 * g + c + 1]
                     nc.tensor.transpose(r_bank[j][g][:, P * c : P * (c + 1)], col.to_broadcast([P, P]), ident[:])
 
         def mean_scalar(i):
@@ -123,43 +157,42 @@ def tile_mix_covariances_of_two_stores_pl_kernel(
         def centre(i, g):
             nc.vector.scalar_tensor_tensor(
                 out=d[i][g][:].rearrange("p (n c) -> p n c", c=4),
-                in0=x[i][:, PASS * g : PASS * (g + 1)].rearrange("p (n c) -> p n c", c=4),
+                in0=x[i][:].rearrange("p (n c) -> p n c", c=8)[:, :, 4 * g : 4 * (g + 1)],
                 scalar=mean[i][:],
                 in1=r_bank[i // 4][g][:].rearrange("p (c n) -> p n c", c=4),
                 op0=ALU.subtract,
                 op1=ALU.mult,
             )
 
-        def turn(i, g):
-            words = d[i][g][:].bitcast(F32)
-            for u in range(2):
+        def turn(i, u):
+            words = d[i][u][:].bitcast(F32)
+            for g in range(2):
                 if i < 7:
                     dst = stage[i][:, P * (2 * g + u) : P * (2 * g + u + 1)]
                 else:
                     dst = last_stage[g][:, P * u : P * (u + 1)]
-                nc.tensor.transpose(dst, words[:, u:256:2], ident[:])
+                nc.tensor.transpose(dst, words[:, P * g : P * (g + 1)], ident[:])
 
-        def copy_out(i):
+        def copy_out(i, copy):
             src = stage[i][:].rearrange("p (g u k) -> p g k u", g=2, u=2)
             if i < 4:
-                dst = gb[i // 2][:].bitcast(F32).rearrange("p (g k u) -> p g k u", g=2, u=2)
-                dst = dst[:, :, P * (i % 2) : P * (i % 2 + 1), :]
+                dst = gb[:].bitcast(F32).rearrange("p (g k u) -> p g k u", g=2, u=2)
+                dst = dst[:, :, P * i : P * (i + 1), :]
             else:
                 dst = ga[i - 4][:].bitcast(F32).rearrange("p (g k u) -> p g k u", g=2, u=2)
-            nc.scalar.copy(out=dst, in_=src)
+            copy(out=dst, in_=src)
 
-        def copy_last(g):
-            nc.scalar.copy(
+        def copy_last(g, copy):
+            copy(
                 out=ga[3][g][:].bitcast(F32).rearrange("p (k u) -> p k u", u=2),
                 in_=last_stage[g][:, 0:256].rearrange("p (u k) -> p k u", u=2),
             )
 
-        def quant_b(pair):
-            for g in range(2):
-                cols = slice(512 * g + 256 * pair, 512 * g + 256 * (pair + 1))
-                nc.vector.quantize_mx(
-                    out=b_codes[:, cols].bitcast(E5M2), scales=b_scale[:, cols], in_=gb[pair][:, 1024 * g : 1024 * (g + 1)]
-                )
+        def quant_b(g):
+            cols = slice(512 * g, 512 * (g + 1))
+            nc.vector.quantize_mx(
+                out=b_codes[:, cols].bitcast(E5M2), scales=b_scale[:, cols], in_=gb[:, 2048 * g : 2048 * (g + 1)]
+            )
 
         def quant_a(r):
             nc.vector.quantize_mx(out=a_codes[r][:].bitcast(E4M3), scales=a_scale[r][:], in_=ga[r][:])
@@ -173,7 +206,7 @@ def tile_mix_covariances_of_two_stores_pl_kernel(
                 j = 4 * z + r
                 nc.tensor.matmul_mx(
                     out=acc[r][:],
-                    lhsT=sa_dealt[:, 256 * j : 256 * (j + 1)].bitcast(E2M1),
+                    lhsT=sa_dealt[r][:, 256 * z : 256 * (z + 1)].bitcast(E2M1),
                     lhsT_scale=sas_dealt[:, P * j : P * (j + 1)],
                     rhs=sbw[:, 512 * z : 512 * (z + 1)].bitcast(E4M3),
                     rhs_scale=sbs[:, 512 * z : 512 * (z + 1)],
@@ -221,93 +254,82 @@ def tile_mix_covariances_of_two_stores_pl_kernel(
         nc.scalar.activation(out=warm[:, 8:9], in_=warm[:, 0:1], func=ACT.Copy, scale=1.0)
         make_identity(nc, ident[:])
         load_r(0, rb)
-        nc.sync.dma_start(
-            out=sa_raw[:].bitcast(I32).rearrange("p (z c) -> p z c", z=2), in_=sa_words.bitcast(I32).rearrange("z p c -> p z c")
-        )
         load_x(0, 0, 512)
         load_x(0, 512, T)
+        load_x(1)
         load_r(1, ra)
-        for i in range(1, 4):
-            load_x(i)
-        load_scales(nc.sync, sas_raw, sa_scales)
+        load_x(2)
+        load_scales(sas_raw, sa_scales, 0)
+        load_scales(sas_raw, sa_scales, 1)
+        load_x(3)
+        load_scales(sas_raw, sa_scales, 2)
+        load_scales(sas_raw, sa_scales, 3)
         load_x(4)
-        load_scales(nc.sync, sbs, sb_scales)
-        nc.sync.dma_start(
-            out=sbw[:].bitcast(I32).rearrange("p (z c) -> p z c", z=2),
-            in_=sb_words.rearrange("z p n t -> p z (n t)").bitcast(I32),
-        )
+        load_sa()
+        load_scales(sbs, sb_scales, 0)
         load_x(5)
+        load_scales(sbs, sb_scales, 1)
+        load_scales(sbs, sb_scales, 2)
+        load_scales(sbs, sb_scales, 3)
+        load_sb()
         load_x(6)
-        load_x(7, 0, 512)
-        load_x(7, 512, T)
-
+        load_x(7)
         spread_r(0)
-        nc.vector.tensor_copy(
-            out=sa_dealt[:].rearrange("p (z r m b) -> p z r m b", z=2, r=4, b=2),
-            in_=sa_raw[:].rearrange("p (z m r b) -> p z r m b", z=2, r=4, b=2),
-        )
         mean_scalar(0)
         mean_vector(0)
         mean_join(0)
-        spread_r(1)
-
-        def tile_front(i):
-            for g in range(2):
-                centre(i, g)
-                turn(i, g)
-
+        deal_scales(nc.gpsimd)
+        for r in (2, 3, 1, 0):
+            deal_words(nc.gpsimd, r)
         mean_scalar(1)
         tile_front(0)
+        spread_r(1)
         mean_scalar(2)
         tile_front(1)
-        copy_out(0)
         mean_scalar(3)
         tile_front(2)
-        copy_out(1)
+        mean_scalar(4)
         tile_front(3)
-        copy_out(2)
-        mean_vector(4)
-        quant_b(0)
-        mean_join(4)
-        nc.vector.tensor_copy(
-            out=sas_dealt[:].rearrange("p (z r m) -> p z r m", z=2, r=4),
-            in_=sas_raw[:].rearrange("p (z m r) -> p z r m", z=2, r=4),
-        )
+        copy_out(0, nc.scalar.copy)
         mean_scalar(5)
-        copy_out(3)
         tile_front(4)
-        stored(0)
+        copy_out(1, nc.vector.tensor_copy)
+        copy_out(2, nc.scalar.copy)
+        copy_out(3, nc.scalar.copy)
+        stored(2)
+        stored(3)
+        centre_both(5)
         stored(1)
+        turn_both(5)
         mean_scalar(6)
-        copy_out(4)
-        tile_front(5)
+        quant_b(0)
         quant_b(1)
+        copy_out(4, nc.scalar.copy)
+        stored(0)
+        copy_out(5, nc.scalar.copy)
+        tile_front(6)
         quant_a(0)
         fresh(0, 0)
         fresh(0, 1)
-        stored(2)
         mean_scalar(7)
-        copy_out(5)
-        tile_front(6)
-        mean_vector(7)
         quant_a(1)
-        mean_join(7)
         fresh(1, 0)
         fresh(1, 1)
-        stored(3)
+        copy_out(6, nc.scalar.copy)
+        tile_front(7)
         evac_scalar(0)
         store_y(0)
-        copy_out(6)
-        tile_front(7)
-        evac_scalar(1)
-        store_y(1)
         quant_a(2)
         fresh(2, 0)
         fresh(2, 1)
-        for g in range(2):
-            copy_last(g)
-            quant_last(g)
-            fresh(3, g)
+        copy_last(0, nc.scalar.copy)
+        copy_last(1, nc.vector.tensor_copy)
+        quant_last(0)
+        quant_last(1)
+        fresh(3, 0)
+        fresh(3, 1)
+        evac_scalar(1)
+        store_y(1)
         evac_vector(2)
         store_y(2)
         evac_scalar(3, 0, 256)

@@ -40,7 +40,8 @@ def tile_mix_covariances_of_two_stores_pl_kernel(
         warm = sbt("warm", 16, F32)
         rcol = [sbt("rcol%d" % j, 8, F32) for j in range(2)]
         x = [sbt("x%d" % i, T, F32) for i in range(8)]
-        d = [[sbt("d%d_%d" % (i, g), PASS, BF16) for g in range(2)] for i in range(8)]
+        d = [[sbt("d%d_%d" % (i, g), PASS, BF16) for g in range(2)] for i in range(7)]
+        d_last = [[sbt("dl%d_%d" % (g, u), 256, BF16) for u in range(2)] for g in range(2)]
         junk_s = [sbt("junk_s%d" % j, T, BF16) for j in range(2)]
         junk_v = sbt("junk_v", PASS, BF16)
         part_s = [sbt("part_s%d" % i, 1, F32) for i in range(8)]
@@ -64,9 +65,9 @@ def tile_mix_covariances_of_two_stores_pl_kernel(
         o_scale = sbt("o_scale", 512, U8)
 
         r_bank = [[bank[0], bank[1]], [bank[2], bank[3]]]
-        stage = [bank[4], bank[5], bank[6], bank[7], bank[4], bank[6], bank[7]]
-        last_stage = [bank[6], bank[2]]
-        acc = [bank[4], bank[5], bank[0], bank[1]]
+        stage = [bank[4], bank[5], bank[6], bank[7], bank[4], bank[7], bank[4]]
+        last_stage = [bank[7], bank[4]]
+        acc = [bank[6], bank[5], bank[0], bank[1]]
 
         xa_dealt = xa.rearrange("(p r) t -> r p t", r=4)
         out_dealt = out_0.rearrange("(p r) n -> r p n", r=4)
@@ -162,6 +163,27 @@ def tile_mix_covariances_of_two_stores_pl_kernel(
                 in1=r_bank[i // 4][g][:].rearrange("p (c n) -> p n c", c=4),
                 op0=ALU.subtract,
                 op1=ALU.mult,
+            )
+
+        def centre_last(g, u):
+            rows_g = slice(64 * g, 64 * (g + 1))
+            nc.vector.scalar_tensor_tensor(
+                out=d_last[g][u][:].rearrange("p (n c) -> p n c", c=4),
+                in0=x[7][:].rearrange("p (n c) -> p n c", c=8)[:, rows_g, 4 * u : 4 * (u + 1)],
+                scalar=mean[7][:],
+                in1=r_bank[1][u][:].rearrange("p (c n) -> p n c", c=4)[:, rows_g, :],
+                op0=ALU.subtract,
+                op1=ALU.mult,
+            )
+
+        def turn_last(g):
+            for u in range(2):
+                nc.tensor.transpose(last_stage[g][:, P * u : P * (u + 1)], d_last[g][u][:].bitcast(F32), ident[:])
+
+        def weave_pair(copy, h, lo, hi):
+            copy(
+                out=yb[:, 4 * lo : 4 * hi].rearrange("p (c i r) -> p c r i", i=4, r=4)[:, :, 2 * h : 2 * h + 2, :],
+                in_=y[:].rearrange("p (r n) -> p r n", r=4)[:, 2 * h : 2 * h + 2, lo:hi].rearrange("p r (c i) -> p c r i", i=4),
             )
 
         def turn(i, u):
@@ -298,14 +320,14 @@ def tile_mix_covariances_of_two_stores_pl_kernel(
         copy_out(3, nc.scalar.copy)
         stored(2)
         stored(3)
-        centre_both(5)
         stored(1)
+        centre_both(5)
         turn_both(5)
+        stored(0)
         mean_scalar(6)
         quant_b(0)
         quant_b(1)
         copy_out(4, nc.scalar.copy)
-        stored(0)
         copy_out(5, nc.scalar.copy)
         tile_front(6)
         quant_a(0)
@@ -316,28 +338,32 @@ def tile_mix_covariances_of_two_stores_pl_kernel(
         fresh(1, 0)
         fresh(1, 1)
         copy_out(6, nc.scalar.copy)
-        tile_front(7)
+        for g in range(2):
+            for u in range(2):
+                centre_last(g, u)
+            turn_last(g)
         evac_scalar(0)
         store_y(0)
+        copy_last(0, nc.scalar.copy)
         quant_a(2)
         fresh(2, 0)
         fresh(2, 1)
-        copy_last(0, nc.scalar.copy)
-        copy_last(1, nc.vector.tensor_copy)
+        copy_last(1, nc.scalar.copy)
         quant_last(0)
         quant_last(1)
         fresh(3, 0)
         fresh(3, 1)
         evac_scalar(1)
         store_y(1)
-        evac_vector(2)
+        weave_pair(nc.vector.tensor_copy, 0, 0, N)
+        evac_scalar(2)
         store_y(2)
         evac_scalar(3, 0, 256)
         evac_scalar(3, 256, N)
         store_y(3)
-        weave(nc.vector.tensor_copy, 0, 256)
-        weave(nc.vector.tensor_copy, 256, 384)
-        weave(nc.scalar.copy, 384, N)
+        weave_pair(nc.vector.tensor_copy, 1, 0, 256)
+        weave_pair(nc.vector.tensor_copy, 1, 256, 384)
+        weave_pair(nc.scalar.copy, 1, 384, N)
         quant_out(0, 256)
         store_codes(0, 256)
         quant_out(256, N)

from contextlib import ExitStack

import concourse.mybir as mybir
from concourse.masks import make_identity

K, N, T, S = 512, 512, 1024, 1024
FLOPS = 2 * K * N * (T + S)

F32 = mybir.dt.float32
BF16 = mybir.dt.bfloat16
I32 = mybir.dt.int32
U32 = mybir.dt.uint32
U8 = mybir.dt.uint8
E4M3 = mybir.dt.float8_e4m3fn_x4
E5M2 = mybir.dt.float8_e5m2_x4
E2M1 = mybir.dt.float4_e2m1fn_x4
ALU = mybir.AluOpType
ACT = mybir.ActivationFunctionType

P = 128
PASS = 512
OUT_SCALE = 0.03
VECTOR_MEAN_COLS = {0: 512}


def tile_mix_covariances_of_two_stores_pl_kernel(
    tc, xa, xb, ra, rb, sa_words, sa_scales, sb_words, sb_scales, out_0, out_1, out_2
):
    nc = tc.nc
    with ExitStack() as ctx:
        sb = ctx.enter_context(tc.tile_pool(name="sb", bufs=1))
        ps = ctx.enter_context(tc.psum_pool(name="ps", bufs=1))
        ctx.enter_context(tc.manual_schedule())

        def sbt(name, cols, dt):
            return sb.tile([P, cols], dt, name=name, align_bytes=64)

        bank = [ps.tile([P, 512], F32, name="bank%d" % j) for j in range(8)]
        ident = sbt("ident", P, F32)
        warm = sbt("warm", 16, F32)
        rcol = [sbt("rcol%d" % j, 8, F32) for j in range(2)]
        x = [sbt("x%d" % i, T, F32) for i in range(8)]
        d = [[sbt("d%d_%d" % (i, g), PASS, BF16) for g in range(2)] for i in range(7)]
        d_last = [[sbt("dl%d_%d" % (g, u), 256, BF16) for u in range(2)] for g in range(2)]
        junk_s = [sbt("junk_s%d" % j, T, BF16) for j in range(2)]
        junk_v = sbt("junk_v", PASS, BF16)
        part_s = [sbt("part_s%d" % i, 1, F32) for i in range(8)]
        part_v = [sbt("part_v%d" % i, 1, F32) for i in range(8)]
        mean = [sbt("mean%d" % i, 1, F32) for i in range(8)]
        gb = sbt("gb", 4096, BF16)
        ga = [[sbt("ga%d_%d" % (r, g), 512, BF16) for g in range(2)] if r == 3 else sbt("ga%d" % r, 1024, BF16) for r in range(4)]
        b_codes = sbt("b_codes", 1024, U32)
        b_scale = sbt("b_scale", 1024, U8)
        a_codes = [sbt("a_codes%d" % r, 256, U32) for r in range(4)]
        a_scale = [sbt("a_scale%d" % r, 256, U8) for r in range(4)]
        sa_raw = sbt("sa_raw", 2048, U8)
        sa_dealt = [sbt("sa_dealt%d" % r, 512, U8) for r in range(4)]
        sas_raw = sbt("sas_raw", 1024, U8)
        sas_dealt = sbt("sas_dealt", 1024, U8)
        sbw = sbt("sbw", 1024, U32)
        sbs = sbt("sbs", 1024, U8)
        y = sbt("y", 2048, F32)
        yb = sbt("yb", 2048, BF16)
        o_codes = sbt("o_codes", 512, U32)
        o_scale = sbt("o_scale", 512, U8)

        r_bank = [[bank[0], bank[1]], [bank[2], bank[3]]]
        stage = [bank[4], bank[5], bank[6], bank[7], bank[4], bank[7], bank[4]]
        last_stage = [bank[7], bank[4]]
        acc = [bank[6], bank[5], bank[0], bank[1]]

        xa_dealt = xa.rearrange("(p r) t -> r p t", r=4)
        out_dealt = out_0.rearrange("(p r) n -> r p n", r=4)

        def rows(i):
            return xb[P * i : P * (i + 1), :] if i < 4 else xa_dealt[i - 4]

        def load_x(i, lo=0, hi=T):
            nc.sync.dma_start(out=x[i][:, lo:hi], in_=rows(i)[:, lo:hi])

        def load_r(j, r):
            nc.sync.dma_start(out=rcol[j][:], in_=r.rearrange("o (p c) -> (o p) c", c=8))

        def load_scales(plane, scales, q):
            nc.sync.dma_start(
                out=plane[32 * q : 32 * q + 4, :].bitcast(I32).rearrange("q (z c) -> q z c", z=2),
                in_=scales[:, 4 * q : 4 * q + 4, :].bitcast(I32).rearrange("z q c -> q z c"),
            )

        def deal_words(eng, r):
            eng.tensor_copy(
                out=sa_dealt[r][:].rearrange("p (m b) -> p m b", b=2),
                in_=sa_raw[:].rearrange("p (m r b) -> p r m b", r=4, b=2)[:, r],
            )

        def deal_scales(eng):
            eng.tensor_copy(
                out=sas_dealt[:].rearrange("p (z r m) -> p z r m", z=2, r=4),
                in_=sas_raw[:].rearrange("p (z m r) -> p z r m", z=2, r=4),
            )

        def load_sa():
            nc.sync.dma_start(
                out=sa_raw[:].bitcast(I32).rearrange("p (z c) -> p z c", z=2),
                in_=sa_words.bitcast(I32).rearrange("z p c -> p z c"),
            )

        def load_sb():
            nc.sync.dma_start(
                out=sbw[:].bitcast(I32).rearrange("p (z c) -> p z c", z=2),
                in_=sb_words.rearrange("z p n t -> p z (n t)").bitcast(I32),
            )

        def centre_both(i):
            for u in range(2):
                centre(i, u)

        def turn_both(i):
            for u in range(2):
                turn(i, u)

        def tile_front(i):
            for u in range(2):
                centre(i, u)
            for u in range(2):
                turn(i, u)

        def spread_r(j):
            for g in range(2):
                for c in range(4):
                    col = rcol[j][:, 4 * g + c : 4 * g + c + 1]
                    nc.tensor.transpose(r_bank[j][g][:, P * c : P * (c + 1)], col.to_broadcast([P, P]), ident[:])

        def mean_scalar(i):
            cols = T - VECTOR_MEAN_COLS.get(i, 0)
            if cols:
                dst = mean[i] if cols == T else part_s[i]
                nc.scalar.activation(
                    out=junk_s[i % 2][:, 0:cols], in_=x[i][:, 0:cols], func=ACT.Copy, scale=1.0 / T, accum_out=dst[:]
                )

        def mean_vector(i):
            v = VECTOR_MEAN_COLS[i]
            lo = T - v
            nc.vector.scalar_tensor_tensor(
                out=junk_v[:, 0 : v // 2], in0=x[i][:, lo : lo + v // 2], scalar=1.0, in1=x[i][:, lo + v // 2 : T],
                op0=ALU.mult, op1=ALU.add, accum_out=part_v[i][:],
            )

        def mean_join(i):
            if VECTOR_MEAN_COLS[i] == T:
                nc.vector.tensor_scalar(out=mean[i][:], in0=part_v[i][:], scalar1=1.0 / T, scalar2=None, op0=ALU.mult)
            else:
                nc.vector.tensor_scalar(
                    out=mean[i][:], in0=part_v[i][:], scalar1=1.0 / T, scalar2=part_s[i][:], op0=ALU.mult, op1=ALU.add
                )

        def centre(i, g):
            nc.vector.scalar_tensor_tensor(
                out=d[i][g][:].rearrange("p (n c) -> p n c", c=4),
                in0=x[i][:].rearrange("p (n c) -> p n c", c=8)[:, :, 4 * g : 4 * (g + 1)],
                scalar=mean[i][:],
                in1=r_bank[i // 4][g][:].rearrange("p (c n) -> p n c", c=4),
                op0=ALU.subtract,
                op1=ALU.mult,
            )

        def centre_last(g, u):
            rows_g = slice(64 * g, 64 * (g + 1))
            nc.vector.scalar_tensor_tensor(
                out=d_last[g][u][:].rearrange("p (n c) -> p n c", c=4),
                in0=x[7][:].rearrange("p (n c) -> p n c", c=8)[:, rows_g, 4 * u : 4 * (u + 1)],
                scalar=mean[7][:],
                in1=r_bank[1][u][:].rearrange("p (c n) -> p n c", c=4)[:, rows_g, :],
                op0=ALU.subtract,
                op1=ALU.mult,
            )

        def turn_last(g):
            for u in range(2):
                nc.tensor.transpose(last_stage[g][:, P * u : P * (u + 1)], d_last[g][u][:].bitcast(F32), ident[:])

        def weave_pair(copy, h, lo, hi):
            copy(
                out=yb[:, 4 * lo : 4 * hi].rearrange("p (c i r) -> p c r i", i=4, r=4)[:, :, 2 * h : 2 * h + 2, :],
                in_=y[:].rearrange("p (r n) -> p r n", r=4)[:, 2 * h : 2 * h + 2, lo:hi].rearrange("p r (c i) -> p c r i", i=4),
            )

        def turn(i, u):
            words = d[i][u][:].bitcast(F32)
            for g in range(2):
                if i < 7:
                    dst = stage[i][:, P * (2 * g + u) : P * (2 * g + u + 1)]
                else:
                    dst = last_stage[g][:, P * u : P * (u + 1)]
                nc.tensor.transpose(dst, words[:, P * g : P * (g + 1)], ident[:])

        def copy_out(i, copy):
            src = stage[i][:].rearrange("p (g u k) -> p g k u", g=2, u=2)
            if i < 4:
                dst = gb[:].bitcast(F32).rearrange("p (g k u) -> p g k u", g=2, u=2)
                dst = dst[:, :, P * i : P * (i + 1), :]
            else:
                dst = ga[i - 4][:].bitcast(F32).rearrange("p (g k u) -> p g k u", g=2, u=2)
            copy(out=dst, in_=src)

        def copy_last(g, copy):
            copy(
                out=ga[3][g][:].bitcast(F32).rearrange("p (k u) -> p k u", u=2),
                in_=last_stage[g][:, 0:256].rearrange("p (u k) -> p k u", u=2),
            )

        def quant_b(g):
            cols = slice(512 * g, 512 * (g + 1))
            nc.vector.quantize_mx(
                out=b_codes[:, cols].bitcast(E5M2), scales=b_scale[:, cols], in_=gb[:, 2048 * g : 2048 * (g + 1)]
            )

        def quant_a(r):
            nc.vector.quantize_mx(out=a_codes[r][:].bitcast(E4M3), scales=a_scale[r][:], in_=ga[r][:])

        def quant_last(g):
            cols = slice(P * g, P * (g + 1))
            nc.vector.quantize_mx(out=a_codes[3][:, cols].bitcast(E4M3), scales=a_scale[3][:, cols], in_=ga[3][g][:])

        def stored(r):
            for z in range(2):
                j = 4 * z + r
                nc.tensor.matmul_mx(
                    out=acc[r][:],
                    lhsT=sa_dealt[r][:, 256 * z : 256 * (z + 1)].bitcast(E2M1),
                    lhsT_scale=sas_dealt[:, P * j : P * (j + 1)],
                    rhs=sbw[:, 512 * z : 512 * (z + 1)].bitcast(E4M3),
                    rhs_scale=sbs[:, 512 * z : 512 * (z + 1)],
                    start=(z == 0),
                    stop=False,
                )

        def fresh(r, g):
            nc.tensor.matmul_mx(
                out=acc[r][:],
                lhsT=a_codes[r][:, P * g : P * (g + 1)].bitcast(E4M3),
                lhsT_scale=a_scale[r][:, P * g : P * (g + 1)],
                rhs=b_codes[:, 512 * g : 512 * (g + 1)].bitcast(E5M2),
                rhs_scale=b_scale[:, 512 * g : 512 * (g + 1)],
                start=False,
                stop=(g == 1),
            )

        def evac_scalar(r, lo=0, hi=N):
            nc.scalar.activation(out=y[:, N * r + lo : N * r + hi], in_=acc[r][:, lo:hi], func=ACT.Copy, scale=OUT_SCALE)

        def evac_vector(r):
            nc.vector.tensor_scalar(out=y[:, N * r : N * (r + 1)], in0=acc[r][:], scalar1=OUT_SCALE, scalar2=None, op0=ALU.mult)

        def store_y(r):
            nc.sync.dma_start(out=out_dealt[r], in_=y[:, N * r : N * (r + 1)])

        def weave(copy, lo, hi):
            copy(
                out=yb[:, 4 * lo : 4 * hi].rearrange("p (c i r) -> p c r i", i=4, r=4),
                in_=y[:].rearrange("p (r n) -> p r n", r=4)[:, :, lo:hi].rearrange("p r (c i) -> p c r i", i=4),
            )

        def quant_out(lo, hi):
            nc.vector.quantize_mx(out=o_codes[:, lo:hi].bitcast(E4M3), scales=o_scale[:, lo:hi], in_=yb[:, 4 * lo : 4 * hi])

        def store_codes(lo, hi):
            nc.sync.dma_start(
                out=out_1[0].rearrange("p n r -> p (n r)")[:, 4 * lo : 4 * hi].bitcast(I32), in_=o_codes[:, lo:hi].bitcast(I32)
            )

        nc.vector.memset(warm[:, 0:1], 0.0)
        nc.vector.memset(sas_raw[:].bitcast(U32), 0)
        nc.vector.memset(sbs[:].bitcast(U32), 0)
        nc.scalar.activation(out=warm[:, 8:9], in_=warm[:, 0:1], func=ACT.Copy, scale=1.0)
        make_identity(nc, ident[:])
        load_r(0, rb)
        load_x(0, 0, 512)
        load_x(0, 512, T)
        load_x(1)
        load_r(1, ra)
        load_x(2)
        load_scales(sas_raw, sa_scales, 0)
        load_scales(sas_raw, sa_scales, 1)
        load_x(3)
        load_scales(sas_raw, sa_scales, 2)
        load_scales(sas_raw, sa_scales, 3)
        load_x(4)
        load_sa()
        load_scales(sbs, sb_scales, 0)
        load_x(5)
        load_scales(sbs, sb_scales, 1)
        load_scales(sbs, sb_scales, 2)
        load_scales(sbs, sb_scales, 3)
        load_sb()
        load_x(6)
        load_x(7)
        spread_r(0)
        mean_scalar(0)
        mean_vector(0)
        mean_join(0)
        deal_scales(nc.gpsimd)
        for r in (2, 3, 1, 0):
            deal_words(nc.gpsimd, r)
        mean_scalar(1)
        tile_front(0)
        spread_r(1)
        mean_scalar(2)
        tile_front(1)
        mean_scalar(3)
        tile_front(2)
        mean_scalar(4)
        tile_front(3)
        copy_out(0, nc.scalar.copy)
        mean_scalar(5)
        tile_front(4)
        copy_out(1, nc.vector.tensor_copy)
        copy_out(2, nc.scalar.copy)
        copy_out(3, nc.scalar.copy)
        stored(2)
        stored(3)
        stored(1)
        centre_both(5)
        turn_both(5)
        stored(0)
        mean_scalar(6)
        quant_b(0)
        quant_b(1)
        copy_out(4, nc.scalar.copy)
        copy_out(5, nc.scalar.copy)
        tile_front(6)
        quant_a(0)
        fresh(0, 0)
        fresh(0, 1)
        mean_scalar(7)
        quant_a(1)
        fresh(1, 0)
        fresh(1, 1)
        copy_out(6, nc.scalar.copy)
        for g in range(2):
            for u in range(2):
                centre_last(g, u)
            turn_last(g)
        evac_scalar(0)
        store_y(0)
        copy_last(0, nc.scalar.copy)
        quant_a(2)
        fresh(2, 0)
        fresh(2, 1)
        copy_last(1, nc.scalar.copy)
        quant_last(0)
        quant_last(1)
        fresh(3, 0)
        fresh(3, 1)
        evac_scalar(1)
        store_y(1)
        weave_pair(nc.vector.tensor_copy, 0, 0, N)
        evac_scalar(2)
        store_y(2)
        evac_scalar(3, 0, 256)
        evac_scalar(3, 256, N)
        store_y(3)
        weave_pair(nc.vector.tensor_copy, 1, 0, 256)
        weave_pair(nc.vector.tensor_copy, 1, 256, 384)
        weave_pair(nc.scalar.copy, 1, 384, N)
        quant_out(0, 256)
        store_codes(0, 256)
        quant_out(256, N)
        store_codes(256, N)
        for q in range(4):
            eng = nc.scalar if q % 2 else nc.sync
            eng.dma_start(out=out_2[0, 4 * q : 4 * q + 4, :].bitcast(I32), in_=o_scale[32 * q : 32 * q + 4, :].bitcast(I32))
